import numpy as np
import ml_dtypes


def mxq(x, axis, fmt="e4m3"):
    dtype, down = {"e4m3": (ml_dtypes.float8_e4m3fn, 7), "e5m2": (ml_dtypes.float8_e5m2, 14)}[fmt]
    v = np.moveaxis(np.asarray(x, np.float32).astype(ml_dtypes.bfloat16).astype(np.float64), axis, -1)
    blocks = v.reshape(v.shape[:-1] + (-1, 32))
    amax = np.abs(blocks).max(-1, keepdims=True)
    byte = np.maximum(np.where(amax > 0, np.frexp(amax)[1] - 1 + 127, 0) - down, 1)
    scale = np.exp2(byte - 127.0)
    codes = (blocks / scale).astype(np.float32).astype(dtype).astype(np.float64)
    return np.moveaxis((codes * scale).reshape(v.shape), -1, axis)


WIDE = False


def mx_kscale(k):
    if not WIDE:
        return np.ones(k)
    levels = np.array([30, -30])
    if k % 512:
        return np.exp2(np.random.permutation(np.resize(levels, k // 32))).repeat(32)
    a = np.empty((k // 512, 16))
    for p in range(k // 512):
        a[p, :8] = np.random.permutation(np.resize(levels, 8))
        for g in range(8):
            far = levels[np.abs(levels - a[p, g]) >= 10]
            a[p, g + 8] = far[np.random.randint(len(far))]
    return np.exp2(a.ravel()).repeat(32)


def f64(x):
    return np.asarray(x).astype(np.float64)


def striped(idx):
    return np.tile(np.asarray(idx).reshape(-1, 16).T, (8, 1)).astype(np.uint16)


def unstriped(offs):
    return offs[:16].T.reshape(-1).astype(np.int64)


def striped8(idx):
    return np.asarray(idx).reshape(8, -1, 16).transpose(0, 2, 1).reshape(128, -1).astype(np.uint16)


def unstriped8(offs):
    return offs.reshape(8, 16, -1).transpose(0, 2, 1).reshape(8, -1).astype(np.int64)


def pick8(x, idx, run):
    r = np.arange(len(x))
    return x[r[:, None], idx[r % (8 * run) // run]]


E2M1 = np.array([0.0, 0.5, 1.0, 1.5, 2.0, 3.0, 4.0, 6.0, -0.0, -0.5, -1.0, -1.5, -2.0, -3.0, -4.0, -6.0])


def pack_weight(w, fmt):
    k, n = w.shape
    w = f64(np.asarray(w, np.float32).astype(ml_dtypes.bfloat16)).reshape(k // 32, 32, n)
    amax = np.abs(w).max(1)
    if fmt in ("e4m3", "e5m2"):
        byte = np.frexp(amax)[1] - 1 + 127 - (7 if fmt == "e4m3" else 14)
    else:
        mant, ex = np.frexp(amax / 6.0)
        byte = np.where(mant > 0.5, ex, ex - 1) + 127
    byte = np.clip(np.where(amax > 0, byte, 1), 1, 254)
    scaled = (w * np.exp2(127.0 - byte)[:, None, :]).reshape(k, n).astype(np.float32)
    by_word = np.ascontiguousarray(scaled.reshape(k // 512, 128, 4, n).transpose(0, 1, 3, 2))
    if fmt in ("e4m3", "e5m2"):
        words = by_word.astype(ml_dtypes.float8_e4m3fn if fmt == "e4m3" else ml_dtypes.float8_e5m2).view(np.uint8)
    else:
        c = by_word.astype(ml_dtypes.float4_e2m1fn).view(np.uint8) & 0xF
        words = (c[..., 0::2] | (c[..., 1::2] << 4)).reshape(k // 512, 128, 2 * n)
    return np.ascontiguousarray(words), np.ascontiguousarray(byte.astype(np.uint8).reshape(k // 512, 16, n))


def unpack_weight(words, scales, fmt):
    g, _, n = scales.shape
    words = np.ascontiguousarray(words).reshape(g, 128, n, -1)
    if fmt in ("e4m3", "e5m2"):
        vals = words.view(ml_dtypes.float8_e4m3fn if fmt == "e4m3" else ml_dtypes.float8_e5m2).astype(np.float64)
    else:
        nib = np.empty((g, 128, n, 4), np.uint8)
        nib[..., 0::2] = words & 0xF
        nib[..., 1::2] = words >> 4
        vals = E2M1[nib]
    vals = vals * np.repeat(np.exp2(scales.astype(np.float64) - 127.0), 8, axis=1)[..., None]
    return vals.transpose(0, 1, 3, 2).reshape(g * 512, n)


K, T, J, R, C, D, I, N = 512, 1024, 256, 512, 512, 512, 256, 256


def setup_inputs():
    n = np.random.standard_normal
    idx = np.random.permutation(T)[:J]
    idx2 = np.stack([np.random.permutation(C)[:J] for _ in range(8)])
    idx3 = np.random.permutation(C)[:I]
    idx4 = np.random.permutation(C)[:I]
    idx5 = np.stack([np.random.permutation(D)[:I] for _ in range(8)])
    fk = mx_kscale(K)
    fr = mx_kscale(R)
    xtp = pack_weight(n((K, T)) / fk[:, None], "e2m1")
    wp = pack_weight(n((K, R)) * 1 / np.sqrt(K) * fk[:, None] * fr, "e5m2")
    wbp = pack_weight(n((R, N)) * 1 / np.sqrt(R) / fr[:, None], "e4m3")
    return {
        "xt_words": xtp[0],
        "xt_scales": xtp[1],
        "w_words": wp[0],
        "w_scales": wp[1],
        "wb_words": wbp[0],
        "wb_scales": wbp[1],
        "offs": striped(idx),
        "offs2": striped8(idx2),
        "offs3": striped(idx3),
        "offs4": striped(idx4),
        "offs5": striped8(idx5),
    }


def reference(xt_words, xt_scales, w_words, w_scales, wb_words, wb_scales, offs, offs2, offs3, offs4, offs5):
    idx = unstriped(offs)
    idx2 = unstriped8(offs2)
    idx3 = unstriped(offs3)
    idx4 = unstriped(offs4)
    idx5 = unstriped8(offs5)
    xtu = unpack_weight(xt_words, xt_scales, "e2m1")
    wu = unpack_weight(w_words, w_scales, "e5m2")
    wbu = unpack_weight(wb_words, wb_scales, "e4m3")
    xtidxg = xtu[:, idx]
    a = wu.T @ xtidxg
    pa = np.zeros((R, C))
    pa[np.arange(R)[:, None], idx2[np.arange(R) % 512 // 64]] = a
    h1 = np.maximum(pa[:, idx3], pa[:, idx4])
    hid = np.zeros((R, D))
    hid[np.arange(R)[:, None], idx5[np.arange(R) % 512 // 64]] = h1
    hidq = mxq(hid, 0, "e5m2")
    p = wbu.T @ hidq
    return p

from contextlib import ExitStack

import concourse.mybir as mybir

K, T, J, R, C, D, I, N = 512, 1024, 256, 512, 512, 512, 256, 256
FLOPS = 2 * K * R * J + 2 * R * N * D

F32 = mybir.dt.float32
BF16 = mybir.dt.bfloat16
I32 = mybir.dt.int32
U32 = mybir.dt.uint32
U16 = mybir.dt.uint16
U8 = mybir.dt.uint8
E2M1 = mybir.dt.float4_e2m1fn_x4
E5M2 = mybir.dt.float8_e5m2_x4
E4M3 = mybir.dt.float8_e4m3fn_x4
COPY = mybir.ActivationFunctionType.Copy
MAX = mybir.AluOpType.max

P = 128
PACK = 4
QUADS = 4
QUAD = P // QUADS
ROWS = 4
CHUNK = 128
HALVES = N // P
HALF = J // 2
REUSED = ("x_word", "w_word", "w_word_dealt", "board0")


def tile_list_mergedstops_kernel(tc, xt_words, xt_scales, w_words, w_scales, wb_words, wb_scales,
                                    offs, offs2, offs3, offs4, offs5, out):
    nc = tc.nc
    with ExitStack() as ctx:
        lists = ctx.enter_context(tc.tile_pool(name="lists", bufs=1))
        sb = ctx.enter_context(tc.tile_pool(name="sb", bufs=1))
        psum = ctx.enter_context(tc.psum_pool(name="psum", bufs=1))

        def load_list(name, source):
            tile = lists.tile([P, source.shape[1]], U16, name=name)
            nc.sync.dma_start(tile[:], source)
            return tile

        def load_scale_rows(plane, source):
            for q in range(QUADS):
                nc.sync.dma_start(plane[QUAD * q : QUAD * q + ROWS, :].bitcast(I32),
                                  source[0, ROWS * q : ROWS * (q + 1), :].bitcast(I32))

        x_scale = sb.tile([P, T], U8, align_bytes=64, tag="x_scale")
        w_scale = sb.tile([P, R], U8, align_bytes=64)
        nc.vector.memset(x_scale[:].bitcast(I32), 0)
        nc.gpsimd.memset(w_scale[:].bitcast(I32), 0)

        token_list = load_list("token_list", offs)
        w_scale_rows = sb.tile([ROWS, QUADS, R // 4], I32, align_bytes=64, tag="w_scale_rows")
        nc.sync.dma_start(w_scale_rows[:], w_scales[0].bitcast(I32).rearrange("(q r) c -> r q c", r=ROWS))
        x_word = sb.tile([P, T], U16, align_bytes=64, tag="x_word")
        w_word = sb.tile([P, R], U32, align_bytes=64, tag="w_word")
        nc.sync.dma_start(w_word[:].bitcast(I32), w_words[0].rearrange("p c t -> p (c t)").bitcast(I32))
        nc.sync.dma_start(x_word[:].bitcast(I32), xt_words[0].bitcast(I32))
        load_scale_rows(x_scale, xt_scales)
        put_first = load_list("put_first", offs2)
        pick_a = load_list("pick_a", offs3)
        pick_b = load_list("pick_b", offs4)
        put_second = load_list("put_second", offs5)

        first_board = [sb.tile([P, C], F32, name=f"first_board{t}", tag=f"board{t}", align_bytes=64) for t in range(PACK)]
        for t in range(PACK):
            (nc.vector if t < PACK // 2 else nc.gpsimd).memset(first_board[t][:], 0.0)

        for q in range(QUADS):
            nc.vector.tensor_copy(w_scale[QUAD * q : QUAD * q + ROWS, :].bitcast(I32), w_scale_rows[:, q, :])

        xg_scale = sb.tile([P, J], U8, align_bytes=64)
        xg_word = sb.tile([P, J], U16, align_bytes=64)
        w_scale_dealt = sb.tile([P, PACK, P], U8, align_bytes=64)
        w_word_dealt = sb.tile([P, PACK, P], U32, align_bytes=64, tag="w_word_dealt")

        def gather(half):
            slots = slice(HALF * half, HALF * (half + 1))
            entries = token_list[:, HALF // 16 * half : HALF // 16 * (half + 1)]
            nc.vector.tensor_copy(xg_word[:, slots], x_word[:].indirect(entries))
            nc.vector.tensor_copy(xg_scale[:, slots], x_scale[:].indirect(entries))

        def deal(t):
            nc.gpsimd.tensor_copy(w_scale_dealt[:, t, :], w_scale[:, t::PACK])
            nc.gpsimd.tensor_copy(w_word_dealt[:, t, :], w_word[:, t::PACK])

        def first_product(t, lo, hi, tag):
            bank = psum.tile([P, hi - lo], F32, name="bank", tag=tag)
            nc.tensor.matmul_mx(out=bank[:], lhsT=w_word_dealt[:, t, :].bitcast(E5M2), lhsT_scale=w_scale_dealt[:, t, :],
                                rhs=xg_word[:, lo:hi].bitcast(E2M1), rhs_scale=xg_scale[:, lo:hi], start=True, stop=True)
            return bank

        def place(t, lo, hi, bank):
            a = sb.tile([P, hi - lo], F32, name=f"a{t}_{lo}")
            if t == 0 and lo == 0:
                nc.scalar.activation(a[:], bank[:], COPY)
            else:
                nc.vector.tensor_copy(a[:], bank[:])
            nc.scalar.activation(first_board[t][:].indirect(put_first[:, lo // 16 : hi // 16]), a[:], COPY)

        deal(0)
        gather(0)
        place(0, 0, HALF, first_product(0, 0, HALF, "bank0"))
        gather(1)
        place(0, HALF, J, first_product(0, HALF, J, "bank4"))
        for t in range(1, PACK):
            deal(t)
            place(t, 0, J, first_product(t, 0, J, f"bank{t}"))

        wb_word = sb.tile([P, N], U32, align_bytes=64, tag="w_scale_rows")
        nc.sync.dma_start(wb_word[:].bitcast(I32), wb_words[0].rearrange("p c t -> p (c t)").bitcast(I32))
        wb_scale = sb.tile([P, N], U8, align_bytes=64, tag="x_scale")
        nc.gpsimd.memset(wb_scale[:].bitcast(I32), 0)
        load_scale_rows(wb_scale, wb_scales)

        kept, second_board = [], []
        for t in range(PACK):
            left = sb.tile([P, I], F32, name=f"left{t}")
            right = sb.tile([P, I], F32, name=f"right{t}")
            h1 = sb.tile([P, I], F32, name=f"h1_{t}")
            nc.vector.tensor_copy(left[:], first_board[t][:].indirect(pick_a[:]))
            nc.vector.tensor_copy(right[:], first_board[t][:].indirect(pick_b[:]))
            nc.vector.tensor_tensor(h1[:], left[:], right[:], MAX)
            kept.append(h1)
            board = sb.tile([P, D], F32, name=f"second_board{t}", tag=REUSED[t], align_bytes=64)
            nc.gpsimd.memset(board[:], 0.0)
            second_board.append(board)

        chunks = D // CHUNK
        woven = [sb.tile([P, CHUNK, PACK], BF16, name=f"woven{c}", align_bytes=64) for c in range(chunks)]

        def weave(t, c):
            nc.vector.tensor_copy(woven[c][:, :, t], second_board[t][:, CHUNK * c : CHUNK * (c + 1)])

        for t in range(PACK):
            nc.scalar.activation(second_board[t][:].indirect(put_second[:]), kept[t][:], COPY)
            if t < PACK - 1:
                for c in range(chunks):
                    weave(t, c)

        out_rows = out.rearrange("(h p) d -> p h d", p=P)

        def finish(c):
            hid_word = sb.tile([P, CHUNK], U32, name=f"hid_word{c}", align_bytes=64)
            hid_scale = sb.tile([P, CHUNK], U8, name=f"hid_scale{c}", align_bytes=64)
            nc.vector.quantize_mx(out=hid_word[:].bitcast(E5M2), scales=hid_scale[:],
                                  in_=woven[c][:].rearrange("p d t -> p (d t)"))
            result = sb.tile([P, HALVES, CHUNK], F32, name=f"result{c}")
            for h in range(HALVES):
                cols = slice(P * h, P * (h + 1))
                bank = psum.tile([P, CHUNK], F32, name="bank", tag=f"bank{HALVES * c + h}")
                nc.tensor.matmul_mx(out=bank[:], lhsT=wb_word[:, cols].bitcast(E4M3), lhsT_scale=wb_scale[:, cols],
                                    rhs=hid_word[:].bitcast(E5M2), rhs_scale=hid_scale[:], start=True, stop=True)
                if c == chunks - 1 and h == 0:
                    nc.vector.tensor_copy(result[:, h, :], bank[:])
                else:
                    nc.scalar.copy(result[:, h, :], bank[:])
            nc.sync.dma_start(out_rows[:, :, CHUNK * c : CHUNK * (c + 1)], result[:])

        weave(PACK - 1, 0)
        for c in range(1, chunks):
            weave(PACK - 1, c)
            finish(c - 1)
        finish(chunks - 1)
